import numpy as np
import ml_dtypes


def mxq(x, axis, fmt="e4m3"):
    dtype, down = {"e4m3": (ml_dtypes.float8_e4m3fn, 7), "e5m2": (ml_dtypes.float8_e5m2, 14)}[fmt]
    v = np.moveaxis(np.asarray(x, np.float32).astype(ml_dtypes.bfloat16).astype(np.float64), axis, -1)
    blocks = v.reshape(v.shape[:-1] + (-1, 32))
    amax = np.abs(blocks).max(-1, keepdims=True)
    byte = np.maximum(np.where(amax > 0, np.frexp(amax)[1] - 1 + 127, 0) - down, 1)
    scale = np.exp2(byte - 127.0)
    codes = (blocks / scale).astype(np.float32).astype(dtype).astype(np.float64)
    return np.moveaxis((codes * scale).reshape(v.shape), -1, axis)


WIDE = False


def mx_kscale(k):
    if not WIDE:
        return np.ones(k)
    levels = np.array([30, -30])
    if k % 512:
        return np.exp2(np.random.permutation(np.resize(levels, k // 32))).repeat(32)
    a = np.empty((k // 512, 16))
    for p in range(k // 512):
        a[p, :8] = np.random.permutation(np.resize(levels, 8))
        for g in range(8):
            far = levels[np.abs(levels - a[p, g]) >= 10]
            a[p, g + 8] = far[np.random.randint(len(far))]
    return np.exp2(a.ravel()).repeat(32)


BF16 = ml_dtypes.bfloat16


def bf(x):
    return np.asarray(x, np.float32).astype(BF16)


def f64(x):
    return np.asarray(x).astype(np.float64)


C, H, W, P, Q = 4, 1024, 1024, 512, 512


def shrink(v, t):
    return np.sign(v) * np.maximum(np.abs(v) - t, 0.0)


def setup_inputs():
    s, u = mx_kscale(W), mx_kscale(H)
    return {"x": bf(np.random.standard_normal((C, H, W)) * s * u[:, None]),
            "b": bf(np.random.standard_normal((W, Q)) / np.sqrt(W) / s[:, None]),
            "sigma": bf((0.5 + 0.4 * np.random.random_sample(H)) * u),
            "tau": bf(0.5 + 0.5 * np.random.random_sample(Q)),
            "a": bf(1.5 * np.random.standard_normal((P, H)) / np.sqrt(H) / u),
            "z0": bf(0.6 * np.random.standard_normal((C, P, Q))),
            "eta": bf(1.0 + 0.1 * np.random.standard_normal((C, P))),
            "lam": bf(0.1 + 0.2 * np.abs(np.random.standard_normal((P, Q))))}


def reference(x, b, sigma, tau, a, z0, eta, lam):
    xq = mxq(f64(x).reshape(C * H, W), 1, "e4m3")
    r = (xq @ mxq(f64(b), 0, "e4m3")).reshape(C, H, Q)
    d = shrink(r, f64(sigma)[:, None] * f64(tau)[None, :])
    dt = d.transpose(1, 0, 2).reshape(H, C * Q)
    y = mxq(f64(a), 1, "e4m3") @ mxq(dt, 0, "e5m2")
    y = y.reshape(P, C, Q).transpose(1, 0, 2)
    return shrink(f64(z0) + f64(eta)[:, :, None] * y, f64(lam))

from contextlib import ExitStack

import concourse.mybir as mybir
from concourse.masks import make_identity

C, H, W, P, Q = 4, 1024, 1024, 512, 512

FLOPS = 2 * C * H * W * Q + 2 * P * H * C * Q

F32 = mybir.dt.float32
BF16 = mybir.dt.bfloat16
U32 = mybir.dt.uint32
U8 = mybir.dt.uint8
E4M3 = mybir.dt.float8_e4m3fn_x4
E5M2 = mybir.dt.float8_e5m2_x4
ALU = mybir.AluOpType
ACT = mybir.ActivationFunctionType

UNITS = 8
VT = {(0, 1), (0, 3), (1, 1), (1, 3)}


def turns(i, half):
    if i == 0:
        return [(1, 0), (1, 1)] if half == 0 else [(1, 2), (1, 3), (2, 0), (2, 1), (2, 2), (2, 3)]
    got = [(i + 2, 2 * half), (i + 2, 2 * half + 1)] if i + 2 < UNITS else []
    if i == 1 and half == 1:
        got = got + [("a", t) for t in range(4)]
    return got


def lessenings(i, half):
    c, odd = divmod(i - 2, 2)
    if i < 2 or i > 7:
        return []
    if i == 2:
        return [(0, 2 * half), (0, 2 * half + 1)]
    if i == 7:
        return [(3, 2 * half), (3, 2 * half + 1)]
    return [((i - 1) // 2, 2 * ((i - 1) % 2) + half)]


def tile_separable_shrinkage_code_f3_kernel(tc, x, b, sigma, tau, a, z0, eta, lam, out):
    nc = tc.nc
    with ExitStack() as ctx:
        keep = ctx.enter_context(tc.tile_pool(name="keep", bufs=1))
        work = ctx.enter_context(tc.tile_pool(name="work", bufs=2))
        psum = ctx.enter_context(tc.psum_pool(name="psum", bufs=2))

        def load_rows(src, name):
            view = src.rearrange("(p t) w -> p t w", t=4)
            halves = []
            for h in (0, 1):
                raw = work.tile([128, 2, 1024], BF16, name="ld", tag="ld", bufs=12)
                nc.sync.dma_start(out=raw[:], in_=view[:, 2 * h : 2 * h + 2, :])
                halves.append(raw)
            return halves

        x_raw = {}
        x_codes = {}
        x_group = {}

        def load_x(i):
            c, g = divmod(i, 2)
            x_raw[i] = load_rows(x[c, 512 * g : 512 * (g + 1), :], "x")

        warm = keep.tile([128, 1], F32, name="warm")
        nc.vector.memset(warm[:], 0.0)
        nc.scalar.activation(out=warm[:], in_=warm[:], func=ACT.Abs)
        ident = keep.tile([128, 128], F32, name="ident")
        make_identity(nc, ident[:])

        load_x(0)
        sig_row = keep.tile([128, H], BF16, name="sig_row")
        nc.gpsimd.memset(sig_row[:], 0.0)
        nc.scalar.dma_start(out=sig_row[0:1, :], in_=sigma.unsqueeze(0))
        tau_row = keep.tile([128, Q], BF16, name="tau_row")
        nc.gpsimd.memset(tau_row[:], 0.0)
        nc.scalar.dma_start(out=tau_row[0:1, :], in_=tau.unsqueeze(0))
        eta_b = keep.tile([128, C, 4], BF16, name="eta_b")
        nc.scalar.dma_start(out=eta_b[:], in_=eta.rearrange("c (p m) -> p c m", m=4))

        b_raw = []
        for k in (0, 1):
            raw = work.tile([128, 4, Q], BF16, name="ld", tag="ld", bufs=12)
            nc.sync.dma_start(out=raw[:], in_=b[512 * k : 512 * (k + 1), :].rearrange("(p j) q -> p j q", j=4))
            b_raw.append(raw)
        load_x(1)
        a_raw = load_rows(a, "a")
        load_x(2)
        lam_t = keep.tile([128, 4, Q], BF16, name="lam_t")
        nc.sync.dma_start(out=lam_t[:], in_=lam.rearrange("(p m) q -> p m q", m=4))
        z0_t = {}

        def load_z0(c):
            z0_t[c] = work.tile([128, 4, Q], BF16, name="z0t", tag="z0t", bufs=4)
            nc.sync.dma_start(out=z0_t[c][:], in_=z0[c].rearrange("(p m) q -> p m q", m=4))

        load_z0(0)
        load_x(3)

        ident_b = keep.tile([128, 128], BF16, name="ident_b")
        nc.gpsimd.tensor_copy(out=ident_b[:], in_=ident[:])
        neg_b = keep.tile([128, 128], BF16, name="neg_b")
        nc.gpsimd.tensor_scalar(out=neg_b[:], in0=ident_b[:], scalar1=-1.0, scalar2=0.0, op0=ALU.mult, op1=ALU.add)
        eta_f = keep.tile([128, C, 4], F32, name="eta_f")
        nc.gpsimd.tensor_copy(out=eta_f[:], in_=eta_b[:])

        th = []

        def make_th(g):
            t_ = keep.tile([128, Q, 4], F32, name="th%d" % g)
            for qq in range(4):
                bank = psum.tile([128, 512], F32, name="rb", tag="rb", bufs=3)
                for t in range(4):
                    nc.tensor.matmul(
                        bank[:, 128 * t : 128 * (t + 1)],
                        lhsT=sig_row[:, 512 * g + t : 512 * (g + 1) : 4],
                        rhs=tau_row[:, 128 * qq : 128 * (qq + 1)],
                        start=True,
                        stop=True,
                    )
                nc.scalar.copy(out=t_[:, 128 * qq : 128 * (qq + 1), :], in_=bank[:].rearrange("p (t q) -> p q t", t=4))
            th.append(t_)

        b_codes, b_scales = [], []

        for k in (0, 1):
            b_codes.append(keep.tile([128, Q], U32, name="bc%d" % k, align_bytes=64))
            b_scales.append(keep.tile([128, Q], U8, name="bs%d" % k, align_bytes=64))

        def prep_b(k, h):
            grp = work.tile([128, 256, 4], BF16, name="bg", tag="bg", bufs=4, align_bytes=64)
            nc.vector.tensor_copy(out=grp[:], in_=b_raw[k][:, :, 256 * h : 256 * (h + 1)].rearrange("p j q -> p q j"))
            return grp

        def quant_b(k, h, grp):
            cols = slice(256 * h, 256 * (h + 1))
            nc.vector.quantize_mx(
                out=b_codes[k][:, cols].bitcast(E4M3), scales=b_scales[k][:, cols], in_=grp[:].rearrange("p q j -> p (q j)")
            )

        def new_group():
            return work.tile([128, 4096], BF16, name="grp", tag="grp", bufs=2, align_bytes=64)

        def turn(raw, t):
            words = raw[t // 2][:, t % 2, :].bitcast(F32)
            bank = psum.tile([128, 512], F32, name="tb", tag="tb", bufs=2)
            for k in (0, 1):
                for u in (0, 1):
                    col = (2 * k + u) * 128
                    nc.tensor.transpose(bank[:, col : col + 128], words[:, 256 * k + u : 256 * (k + 1) : 2], ident[:])
            return bank

        def copy_turned(bank, grp, t, on_vector):
            dst = grp[:].bitcast(F32)[:, 512 * t : 512 * (t + 1)].rearrange("k (g p u) -> k g p u", g=2, u=2)
            src = bank[:].rearrange("k (g u p) -> k g p u", g=2, u=2)
            if on_vector:
                nc.vector.tensor_copy(out=dst, in_=src)
            else:
                nc.scalar.copy(out=dst, in_=src)

        def quant_rows(grp, codes, scales, half):
            lo, hi = 2048 * half, 2048 * (half + 1)
            nc.vector.quantize_mx(
                out=codes[:, lo // 4 : hi // 4].bitcast(E4M3), scales=scales[:, lo // 4 : hi // 4], in_=grp[:, lo:hi]
            )

        def turn_x(i, t, on_vector=False):
            if t == 0:
                x_group[i] = new_group()
            copy_turned(turn(x_raw[i], t), x_group[i], t, on_vector)

        def quant_x(i, half):
            if half == 0:
                x_codes[i] = (
                    work.tile([128, 1024], U32, name="xc", tag="xc", bufs=3, align_bytes=64),
                    work.tile([128, 1024], U8, name="xs", tag="xs", bufs=3, align_bytes=64),
                )
            quant_rows(x_group[i], x_codes[i][0], x_codes[i][1], half)

        mag, sgn = {}, {}

        def stage1(i, qq):
            bank = psum.tile([128, 512], F32, name="rb", tag="rb", bufs=3)
            codes, scales = x_codes[i]
            q_cols = slice(128 * qq, 128 * (qq + 1))
            for t in range(4):
                for k in (0, 1):
                    cols = slice((2 * t + k) * 128, (2 * t + k + 1) * 128)
                    nc.tensor.matmul_mx(
                        out=bank[:, 128 * t : 128 * (t + 1)],
                        lhsT=codes[:, cols].bitcast(E4M3),
                        lhsT_scale=scales[:, cols],
                        rhs=b_codes[k][:, q_cols].bitcast(E4M3),
                        rhs_scale=b_scales[k][:, q_cols],
                        start=(k == 0),
                        stop=(k == 1),
                    )
            h = qq // 2
            if qq % 2 == 0:
                mag[i, h] = work.tile([128, 256, 4], F32, name="mag", tag="mag", bufs=4)
                sgn[i, h] = work.tile([128, 256, 4], BF16, name="sgn", tag="sgn", bufs=4)
            dst = slice(128 * (qq % 2), 128 * (qq % 2 + 1))
            src = bank[:].rearrange("p (t q) -> p q t", t=4)
            nc.scalar.activation(out=mag[i, h][:, dst, :], in_=src, func=ACT.Abs)
            nc.scalar.activation(out=sgn[i, h][:, dst, :], in_=src, func=ACT.Sign)

        exc, d_in, d_codes = {}, {}, {}

        def over(i, h):
            exc[i, h] = work.tile([128, 256, 4], BF16, name="exc", tag="exc", bufs=3)
            nc.vector.tensor_tensor(
                out=exc[i, h][:], in0=mag[i, h][:], in1=th[i % 2][:, 256 * h : 256 * (h + 1), :], op=ALU.subtract
            )

        def clip0(i, h):
            nc.vector.tensor_scalar(out=exc[i, h][:], in0=exc[i, h][:], scalar1=0.0, scalar2=None, op0=ALU.max)

        def signed(i, h):
            if h == 0:
                d_in[i] = work.tile([128, 2048], BF16, name="d_in", tag="d_in", bufs=2, align_bytes=64)
            nc.vector.tensor_tensor(
                out=d_in[i][:, 1024 * h : 1024 * (h + 1)],
                in0=exc[i, h][:].rearrange("p q t -> p (q t)"),
                in1=sgn[i, h][:].rearrange("p q t -> p (q t)"),
                op=ALU.mult,
            )

        def quant_d(i):
            codes = work.tile([128, Q], U32, name="dc", tag="dc", bufs=4, align_bytes=64)
            scales = work.tile([128, Q], U8, name="ds", tag="ds", bufs=4, align_bytes=64)
            nc.vector.quantize_mx(out=codes[:].bitcast(E5M2), scales=scales[:], in_=d_in[i][:])
            d_codes[i] = (codes, scales)

        a_codes = keep.tile([128, 1024], U32, name="ac", align_bytes=64)
        a_scales = keep.tile([128, 1024], U8, name="as_", align_bytes=64)
        lam2 = keep.tile([128, 4, Q], BF16, name="lam2")
        less = {}
        y_bank, u1, u2, z_t = {}, {}, {}, {}

        def z0_less_lam(c, m):
            if m == 0:
                less[c] = work.tile([128, 4, Q], F32, name="less", tag="less", bufs=2)
            if (c, m) == (3, 3):
                nc.gpsimd.tensor_tensor(out=less[c][:, m, :], in0=z0_t[c][:, m, :], in1=lam_t[:, m, :], op=ALU.subtract)
                return
            bank = psum.tile([128, Q], F32, name="eb", tag="eb", bufs=1)
            nc.tensor.matmul(bank[:], lhsT=ident_b[:], rhs=z0_t[c][:, m, :], start=True, stop=False)
            nc.tensor.matmul(bank[:], lhsT=neg_b[:], rhs=lam_t[:, m, :], start=False, stop=True)
            nc.scalar.copy(out=less[c][:, m, :], in_=bank[:])

        def stage2(c, m):
            bank = psum.tile([128, Q], F32, name="yb", tag="yb", bufs=2)
            for g in (0, 1):
                cols = slice((2 * m + g) * 128, (2 * m + g + 1) * 128)
                codes, scales = d_codes[2 * c + g]
                nc.tensor.matmul_mx(
                    out=bank[:],
                    lhsT=a_codes[:, cols].bitcast(E4M3),
                    lhsT_scale=a_scales[:, cols],
                    rhs=codes[:].bitcast(E5M2),
                    rhs_scale=scales[:],
                    start=(g == 0),
                    stop=(g == 1),
                )
            y_bank[c, m] = bank

        def step_u1(c, m):
            u1[c, m] = work.tile([128, Q], F32, name="u1", tag="u1", bufs=4)
            nc.vector.scalar_tensor_tensor(
                out=u1[c, m][:], in0=y_bank[c, m][:], scalar=eta_f[:, c, m : m + 1], in1=less[c][:, m, :],
                op0=ALU.mult, op1=ALU.add,
            )

        def step_u2(c, m):
            u2[c, m] = work.tile([128, Q], F32, name="u2", tag="u2", bufs=2)
            nc.vector.tensor_tensor(out=u2[c, m][:], in0=u1[c, m][:], in1=lam2[:, m, :], op=ALU.add)

        def step_z(c, m):
            if m % 2 == 0:
                z_t[c, m // 2] = work.tile([128, 2, Q], F32, name="zt", tag="zt", bufs=3)
            zt = z_t[c, m // 2]
            nc.vector.scalar_tensor_tensor(
                out=zt[:, m % 2, :], in0=u2[c, m][:], scalar=0.0, in1=u1[c, m][:], op0=ALU.min, op1=ALU.max
            )
            if m % 2 == 1:
                nc.sync.dma_start(out=out[c].rearrange("(p m) q -> p m q", m=4)[:, m - 1 : m + 1, :], in_=zt[:])

        def stage2_group(c, ms, mid):
            for m in ms:
                stage2(c, m)
            for m in ms:
                step_u1(c, m)
            if mid is not None:
                mid()
            for m in ms:
                step_u2(c, m)
            for m in ms:
                step_z(c, m)

        def vec_turn(i, t):
            return (i, t) in VT

        turn_x(0, 0, vec_turn(0, 0))
        turn_x(0, 1, vec_turn(0, 1))
        g00 = prep_b(0, 0)
        g01 = prep_b(0, 1)
        turn_x(0, 2, vec_turn(0, 2))
        turn_x(0, 3, vec_turn(0, 3))
        quant_x(0, 0)
        quant_b(0, 0, g00)
        make_th(0)
        g10 = prep_b(1, 0)
        quant_x(0, 1)
        quant_b(1, 0, g10)
        g11 = prep_b(1, 1)
        quant_b(0, 1, g01)
        quant_b(1, 1, g11)
        def turn_some(pairs):
            for i, t in pairs:
                if i == "a":
                    if t == 0:
                        x_group["a"] = new_group()
                    copy_turned(turn(a_raw, t), x_group["a"], t, (i, t) in VT)
                else:
                    turn_x(i, t, (i, t) in VT)

        for i in range(UNITS + 1):
            j = i - 1
            nxt = i + 1
            if i + 4 < UNITS:
                load_x(i + 4)
            if i in (1, 3, 5):
                load_z0((i + 1) // 2)
            if j >= 0:
                over(j, 1)
            if i < UNITS:
                stage1(i, 0)
                stage1(i, 1)
            if 1 <= i and nxt < UNITS:
                quant_x(nxt, 0)
            if j >= 0:
                clip0(j, 1)
            if 1 <= i and nxt < UNITS:
                quant_x(nxt, 1)
            if j >= 0:
                signed(j, 1)
            turn_some(turns(i, 0))
            if 2 <= i:
                for c, m in lessenings(i, 0):
                    z0_less_lam(c, m)
            if i >= 3 and i % 2 == 1:
                stage2_group((i - 3) // 2, (2, 3), lambda: quant_d(j))
            elif j >= 0:
                quant_d(j)
            if i < UNITS:
                over(i, 0)
                stage1(i, 2)
                stage1(i, 3)
                clip0(i, 0)
            if i == 0:
                make_th(1)
            turn_some(turns(i, 1))
            for c, m in lessenings(i, 1):
                z0_less_lam(c, m)
            if i == 0:
                quant_x(1, 0)
                quant_x(1, 1)
            if i == 1:
                for h in (0, 1):
                    quant_rows(x_group["a"], a_codes, a_scales, h)
                nc.vector.tensor_scalar(out=lam2[:], in0=lam_t[:], scalar1=2.0, scalar2=None, op0=ALU.mult)
            if i >= 2 and i % 2 == 0:
                mid = (lambda: signed(i, 0)) if i < UNITS else None
                stage2_group((i - 2) // 2, (0, 1), mid)
            elif i < UNITS:
                signed(i, 0)
        stage2_group(3, (2, 3), None)
